import numpy as np
import ml_dtypes


def mxq(x, axis, fmt="e4m3"):
    dtype, down = {"e4m3": (ml_dtypes.float8_e4m3fn, 7), "e5m2": (ml_dtypes.float8_e5m2, 14)}[fmt]
    v = np.moveaxis(np.asarray(x, np.float32).astype(ml_dtypes.bfloat16).astype(np.float64), axis, -1)
    blocks = v.reshape(v.shape[:-1] + (-1, 32))
    amax = np.abs(blocks).max(-1, keepdims=True)
    byte = np.maximum(np.where(amax > 0, np.frexp(amax)[1] - 1 + 127, 0) - down, 1)
    scale = np.exp2(byte - 127.0)
    codes = (blocks / scale).astype(np.float32).astype(dtype).astype(np.float64)
    return np.moveaxis((codes * scale).reshape(v.shape), -1, axis)


WIDE = False


def mx_kscale(k):
    if not WIDE:
        return np.ones(k)
    levels = np.array([10, -10, 5, -5, 0])
    if k % 512:
        return np.exp2(np.random.permutation(np.resize(levels, k // 32))).repeat(32)
    a = np.empty((k // 512, 16))
    for p in range(k // 512):
        a[p, :8] = np.random.permutation(np.resize(levels, 8))
        for g in range(8):
            far = levels[np.abs(levels - a[p, g]) >= 10]
            a[p, g + 8] = far[np.random.randint(len(far))]
    return np.exp2(a.ravel()).repeat(32)


def f64(x):
    return np.asarray(x).astype(np.float64)


E2M1 = np.array([0.0, 0.5, 1.0, 1.5, 2.0, 3.0, 4.0, 6.0, -0.0, -0.5, -1.0, -1.5, -2.0, -3.0, -4.0, -6.0])


def pack_weight(w, fmt):
    k, n = w.shape
    w = f64(np.asarray(w, np.float32).astype(ml_dtypes.bfloat16)).reshape(k // 32, 32, n)
    amax = np.abs(w).max(1)
    if fmt == "e4m3":
        byte = np.frexp(amax)[1] - 1 + 127 - 7
    else:
        mant, ex = np.frexp(amax / 6.0)
        byte = np.where(mant > 0.5, ex, ex - 1) + 127
    byte = np.clip(np.where(amax > 0, byte, 1), 1, 254)
    scaled = (w * np.exp2(127.0 - byte)[:, None, :]).reshape(k, n).astype(np.float32)
    by_word = np.ascontiguousarray(scaled.reshape(k // 512, 128, 4, n).transpose(0, 1, 3, 2))
    if fmt == "e4m3":
        words = by_word.astype(ml_dtypes.float8_e4m3fn).view(np.uint8)
    else:
        c = by_word.astype(ml_dtypes.float4_e2m1fn).view(np.uint8) & 0xF
        words = (c[..., 0::2] | (c[..., 1::2] << 4)).reshape(k // 512, 128, 2 * n)
    return np.ascontiguousarray(words), np.ascontiguousarray(byte.astype(np.uint8).reshape(k // 512, 16, n))


def unpack_weight(words, scales, fmt):
    g, _, n = scales.shape
    words = np.ascontiguousarray(words).reshape(g, 128, n, -1)
    if fmt == "e4m3":
        vals = words.view(ml_dtypes.float8_e4m3fn).astype(np.float64)
    else:
        nib = np.empty((g, 128, n, 4), np.uint8)
        nib[..., 0::2] = words & 0xF
        nib[..., 1::2] = words >> 4
        vals = E2M1[nib]
    vals = vals * np.repeat(np.exp2(scales.astype(np.float64) - 127.0), 8, axis=1)[..., None]
    return vals.transpose(0, 1, 3, 2).reshape(g * 512, n)


K, L, M, T, B, N = 1024, 512, 512, 1024, 128, 512


def setup_inputs():
    n = np.random.standard_normal
    fk = mx_kscale(K)
    fl = mx_kscale(L)
    fm = mx_kscale(M)
    xtp = pack_weight(n((K, T)) / fk[:, None], "e4m3")
    xqp = pack_weight(n((L, T)) / fl[:, None], "e2m1")
    wqp = pack_weight(n((L, N)) * 1 / np.sqrt(L) * fl[:, None], "e4m3")
    xgp = pack_weight(n((M, B)) / fm[:, None], "e4m3")
    wgp = pack_weight(n((M, N)) * 1 / np.sqrt(M) * fm[:, None], "e4m3")
    return {
        "xt_words": xtp[0],
        "xt_scales": xtp[1],
        "wa": (n((K, N)) * 1 / np.sqrt(K) * fk[:, None]).astype(np.float32),
        "xq_words": xqp[0],
        "xq_scales": xqp[1],
        "wq_words": wqp[0],
        "wq_scales": wqp[1],
        "xg_words": xgp[0],
        "xg_scales": xgp[1],
        "wg_words": wgp[0],
        "wg_scales": wgp[1],
    }


def reference(xt_words, xt_scales, wa, xq_words, xq_scales, wq_words, wq_scales, xg_words, xg_scales, wg_words, wg_scales):
    xtu = unpack_weight(xt_words, xt_scales, "e4m3")
    xqu = unpack_weight(xq_words, xq_scales, "e2m1")
    wqu = unpack_weight(wq_words, wq_scales, "e4m3")
    xgu = unpack_weight(xg_words, xg_scales, "e4m3")
    wgu = unpack_weight(wg_words, wg_scales, "e4m3")
    waq = mxq(f64(wa), 0, "e4m3")
    z = waq.T @ xtu + wqu.T @ xqu
    u = z.reshape(N, B, T // B).max(axis=2)
    g = wgu.T @ xgu
    y = u - np.mean(z, axis=1, keepdims=True) + 0.5 * g
    return y

@@ -1,0 +1,232 @@
+from contextlib import ExitStack
+
+import concourse.mybir as mybir
+
+K, L, M, T, B, N = 1024, 512, 512, 1024, 128, 512
+FLOPS = 2 * N * T * (K + L) + 2 * N * B * M
+
+F32 = mybir.dt.float32
+BF16 = mybir.dt.bfloat16
+I32 = mybir.dt.int32
+U32 = mybir.dt.uint32
+U8 = mybir.dt.uint8
+FP8X4 = mybir.dt.float8_e4m3fn_x4
+FP4X4 = mybir.dt.float4_e2m1fn_x4
+ALU = mybir.AluOpType
+ACT = mybir.ActivationFunctionType
+
+P = 128
+PACK = 4
+GROUP = T // B
+HALF = 512
+TILES = N // P
+N_HALF = N // 2
+V_COLS = 336
+XT_ROW = 4
+G_ROW = 8
+
+
+def tile_mix_peak_of_mixed_sum_kernel(
+    tc, xt_words, xt_scales, wa, xq_words, xq_scales, wq_words, wq_scales,
+    xg_words, xg_scales, wg_words, wg_scales, out,
+):
+    nc = tc.nc
+    with ExitStack() as ctx:
+        sb = ctx.enter_context(tc.tile_pool(name="sb", bufs=1))
+        ps = ctx.enter_context(tc.psum_pool(name="ps", bufs=1))
+        ctx.enter_context(tc.manual_schedule())
+
+        def sbuf(name, shape, dtype):
+            return sb.tile(shape, dtype, name=name, align_bytes=64)
+
+        wq_plane = sbuf("wq_plane", [P, N], U8)
+        xq_plane = sbuf("xq_plane", [P, T], U8)
+        xt_plane = sbuf("xt_plane", [P, 2 * T], U8)
+        wg_plane = sbuf("wg_plane", [P, N], U8)
+        xg_plane = sbuf("xg_plane", [P, B], U8)
+        for plane in (wq_plane, xq_plane, xt_plane, wg_plane, xg_plane):
+            nc.vector.memset(plane[:].bitcast(I32), 0)
+
+        warm_in = sbuf("warm_in", [P, 1], F32)
+        warm_out = sbuf("warm_out", [P, 1], F32)
+        nc.vector.memset(warm_in[:], 0.0)
+        nc.scalar.activation(warm_out[:], warm_in[:], ACT.Copy)
+
+        def scale_rows(plane, scales, first_row):
+            passes = scales.shape[0]
+            rows = scales.bitcast(I32).rearrange("g (q r) c -> r q g c", r=4)
+            dst = plane[:].bitcast(I32).rearrange("p (g c) -> p g c", g=passes)
+            return [(dst[first_row + r : P : 32], rows[r]) for r in range(4)]
+
+        scale_loads = (
+            scale_rows(wq_plane, wq_scales, 0)
+            + scale_rows(xq_plane, xq_scales, 0)
+            + scale_rows(xt_plane, xt_scales, XT_ROW)
+            + scale_rows(wg_plane, wg_scales, G_ROW)
+            + scale_rows(xg_plane, xg_scales, G_ROW)
+        )
+
+        def load_scales(engine, first, last):
+            for dst, src in scale_loads[first:last]:
+                engine.dma_start(out=dst, in_=src)
+
+        def load_words(name, words):
+            t = sbuf(name, [P, words.shape[1]], U32)
+            nc.sync.dma_start(out=t[:].bitcast(I32), in_=words)
+            return t
+
+        def as_words(words):
+            return words.rearrange("g p c r -> g p (c r)").bitcast(I32)
+
+        wa_rows = wa.rearrange("(g p j) n -> g p j n", p=P, j=PACK)
+        wa_raw = [sbuf("wa_raw%d" % g, [P, PACK, N], F32) for g in range(2)]
+        xt_w = as_words(xt_words)
+
+        nc.sync.dma_start(out=wa_raw[0][:, 0:2, :], in_=wa_rows[0][:, 0:2, :])
+        load_scales(nc.sync, 0, 4)
+        nc.sync.dma_start(out=wa_raw[0][:, 2:4, :], in_=wa_rows[0][:, 2:4, :])
+        wq_codes = load_words("wq_codes", as_words(wq_words)[0])
+        xq_codes = sbuf("xq_codes", [P, 2 * T], U8)
+        nc.sync.dma_start(out=xq_codes[:].bitcast(I32), in_=xq_words[0].bitcast(I32))
+        load_scales(nc.sync, 4, 8)
+        nc.sync.dma_start(out=wa_raw[1][:], in_=wa_rows[1])
+        load_scales(nc.sync, 8, 12)
+        xt00 = load_words("xt00", xt_w[0][:, 0:HALF])
+        xt10 = load_words("xt10", xt_w[1][:, 0:HALF])
+        xt_h1 = sbuf("xt_h1", [P, 2, HALF], U32)
+        nc.sync.dma_start(out=xt_h1[:].bitcast(I32), in_=xt_w.rearrange("g p c -> p g c")[:, :, HALF:T])
+        load_scales(nc.sync, 12, 16)
+        wg_codes = load_words("wg_codes", as_words(wg_words)[0])
+        xg_codes = load_words("xg_codes", as_words(xg_words)[0])
+        load_scales(nc.sync, 16, 20)
+        xt_codes = {(0, 0): xt00[:], (1, 0): xt10[:], (0, 1): xt_h1[:, 0, :], (1, 1): xt_h1[:, 1, :]}
+
+        wa_codes, wa_plane = {}, {}
+
+        def quantize_wa(g):
+            grouped = sbuf("wa_bf16_%d" % g, [P, N, PACK], BF16)
+
+            def views(c0, c1):
+                return (
+                    grouped[:, c0:c1, :].rearrange("p (c i) j -> p c j i", i=4),
+                    wa_raw[g][:, :, c0:c1].rearrange("p j (c i) -> p c j i", i=4),
+                )
+
+            nc.vector.tensor_copy(*views(0, N_HALF))
+            nc.scalar.copy(*views(V_COLS, N))
+            nc.vector.tensor_copy(*views(N_HALF, V_COLS))
+            for u in range(2):
+                wa_codes[g, u] = sbuf("wa_codes%d%d" % (g, u), [P, N_HALF], U32)
+                wa_plane[g, u] = sbuf("wa_plane%d%d" % (g, u), [P, N_HALF], U8)
+                nc.vector.quantize_mx(
+                    out=wa_codes[g, u][:].bitcast(FP8X4),
+                    scales=wa_plane[g, u][:],
+                    in_=grouped[:, u * N_HALF : (u + 1) * N_HALF, :].rearrange("p c j -> p (c j)"),
+                )
+
+        banks = [(h, j) for h in range(2) for j in range(TILES)]
+        z = {}
+        for h, j in banks:
+            z[h, j] = ps.tile([P, HALF], F32, name="z%d%d" % (h, j), tag="bank%d%d" % (h, j))
+
+        def xq_pass(h, j):
+            cols = slice(j * P, (j + 1) * P)
+            nc.tensor.matmul_mx(
+                out=z[h, j][:],
+                lhsT=wq_codes[:, cols].bitcast(FP8X4),
+                lhsT_scale=wq_plane[:, cols],
+                rhs=xq_codes[:, 2 * h * HALF : 2 * (h + 1) * HALF].bitcast(FP4X4),
+                rhs_scale=xq_plane[:, h * HALF : (h + 1) * HALF],
+                start=True,
+                stop=False,
+            )
+
+        def xt_pass(g, h, j):
+            u, c0 = divmod(j * P, N_HALF)
+            t0 = g * T + h * HALF
+            nc.tensor.matmul_mx(
+                out=z[h, j][:],
+                lhsT=wa_codes[g, u][:, c0 : c0 + P].bitcast(FP8X4),
+                lhsT_scale=wa_plane[g, u][:, c0 : c0 + P],
+                rhs=xt_codes[g, h].bitcast(FP8X4),
+                rhs_scale=xt_plane[XT_ROW:P, t0 : t0 + HALF],
+                start=False,
+                stop=(g == 1),
+            )
+
+        for h, j in banks:
+            xq_pass(h, j)
+        quantize_wa(0)
+        quantize_wa(1)
+        for g in range(2):
+            for j in range(2):
+                xt_pass(g, 0, j)
+        for h, j in banks[2:-1]:
+            for g in range(2):
+                xt_pass(g, h, j)
+
+        peaks = sbuf("peaks", [P, TILES, B], F32)
+        neg_mean = sbuf("neg_mean", [P, 2 * TILES], F32)
+        scaled = sbuf("scaled", [P, 2 * TILES, HALF], BF16)
+        groups = HALF // GROUP
+
+        def peak(h, j):
+            nc.vector.tensor_reduce(
+                out=peaks[:, j, h * groups : (h + 1) * groups],
+                in_=z[h, j][:].rearrange("p (b e) -> p b e", e=GROUP),
+                axis=mybir.AxisListType.X,
+                op=ALU.max,
+            )
+
+        def total(h, j):
+            i = h * TILES + j
+            if h == 0:
+                nc.scalar.activation(
+                    scaled[:, i, :], z[h, j][:], ACT.Copy, scale=-1.0 / (T * HALF), accum_out=neg_mean[:, i : i + 1]
+                )
+            else:
+                nc.scalar.activation(
+                    scaled[:, i, :], z[h, j][:], ACT.Identity, scale=-1.0 / T, bias=neg_mean[:, j : j + 1],
+                    accum_out=neg_mean[:, i : i + 1],
+                )
+
+        def pair(h, j):
+            peak(h, j)
+            total(h, j + 1)
+            peak(h, j + 1)
+            total(h, j)
+
+        pair(0, 0)
+        gsum = ps.tile([P, TILES, B], F32, name="gsum", tag="bank00")
+        for j in range(TILES):
+            cols = slice(j * P, (j + 1) * P)
+            nc.tensor.matmul_mx(
+                out=gsum[:, j, :],
+                lhsT=wg_codes[:, cols].bitcast(FP8X4),
+                lhsT_scale=wg_plane[G_ROW:P, cols],
+                rhs=xg_codes[:].bitcast(FP8X4),
+                rhs_scale=xg_plane[G_ROW:P, :],
+                start=True,
+                stop=True,
+            )
+        for g in range(2):
+            xt_pass(g, 1, TILES - 1)
+        pair(0, 2)
+        pair(1, 0)
+
+        half_g = sbuf("half_g", [P, TILES, B], F32)
+        result = sbuf("result", [P, TILES, B], F32)
+        nc.scalar.activation(half_g[:], gsum[:], ACT.Copy, scale=0.5)
+
+        def finish(j):
+            nc.vector.scalar_tensor_tensor(
+                out=result[:, j, :], in0=peaks[:, j, :], scalar=neg_mean[:, TILES + j : TILES + j + 1],
+                in1=half_g[:, j, :], op0=ALU.add, op1=ALU.add,
+            )
+            nc.sync.dma_start(out=out[j * P : (j + 1) * P, :], in_=result[:, j, :])
+
+        for j in (2, 3):
+            peak(1, j)
+            total(1, j)
+        for j in range(TILES):
+            finish(j)

@@ -24,6 +24,7 @@ N_HALF = N // 2
 V_COLS = 336
 XT_ROW = 4
 G_ROW = 8
+WARM_PASSES = 3
 
 
 def tile_mix_peak_of_mixed_sum_kernel(
@@ -44,12 +45,12 @@ def tile_mix_peak_of_mixed_sum_kernel(
         xt_plane = sbuf("xt_plane", [P, 2 * T], U8)
         wg_plane = sbuf("wg_plane", [P, N], U8)
         xg_plane = sbuf("xg_plane", [P, B], U8)
-        for plane in (wq_plane, xq_plane, xt_plane, wg_plane, xg_plane):
+        for plane in (wq_plane, xt_plane, xq_plane, xg_plane, wg_plane):
             nc.vector.memset(plane[:].bitcast(I32), 0)
 
         warm_in = sbuf("warm_in", [P, 1], F32)
         warm_out = sbuf("warm_out", [P, 1], F32)
-        nc.vector.memset(warm_in[:], 0.0)
+        nc.gpsimd.memset(warm_in[:], 0.0)
         nc.scalar.activation(warm_out[:], warm_in[:], ACT.Copy)
 
         def scale_rows(plane, scales, first_row):
@@ -84,13 +85,14 @@ def tile_mix_peak_of_mixed_sum_kernel(
 
         nc.sync.dma_start(out=wa_raw[0][:, 0:2, :], in_=wa_rows[0][:, 0:2, :])
         load_scales(nc.sync, 0, 4)
-        nc.sync.dma_start(out=wa_raw[0][:, 2:4, :], in_=wa_rows[0][:, 2:4, :])
         wq_codes = load_words("wq_codes", as_words(wq_words)[0])
         xq_codes = sbuf("xq_codes", [P, 2 * T], U8)
         nc.sync.dma_start(out=xq_codes[:].bitcast(I32), in_=xq_words[0].bitcast(I32))
+        nc.sync.dma_start(out=wa_raw[0][:, 2:4, :], in_=wa_rows[0][:, 2:4, :])
         load_scales(nc.sync, 4, 8)
         nc.sync.dma_start(out=wa_raw[1][:], in_=wa_rows[1])
-        load_scales(nc.sync, 8, 12)
+        load_scales(nc.gpsimd, 8, 12)
+        load_scales(nc.sync, 16, 20)
         xt00 = load_words("xt00", xt_w[0][:, 0:HALF])
         xt10 = load_words("xt10", xt_w[1][:, 0:HALF])
         xt_h1 = sbuf("xt_h1", [P, 2, HALF], U32)
@@ -98,7 +100,6 @@ def tile_mix_peak_of_mixed_sum_kernel(
         load_scales(nc.sync, 12, 16)
         wg_codes = load_words("wg_codes", as_words(wg_words)[0])
         xg_codes = load_words("xg_codes", as_words(xg_words)[0])
-        load_scales(nc.sync, 16, 20)
         xt_codes = {(0, 0): xt00[:], (1, 0): xt10[:], (0, 1): xt_h1[:, 0, :], (1, 1): xt_h1[:, 1, :]}
 
         wa_codes, wa_plane = {}, {}
@@ -154,6 +155,16 @@ def tile_mix_peak_of_mixed_sum_kernel(
                 stop=(g == 1),
             )
 
+        for h, j in banks[-WARM_PASSES:]:
+            nc.tensor.matmul_mx(
+                out=z[h, j][:],
+                lhsT=wq_codes[:, 0:P].bitcast(FP8X4),
+                lhsT_scale=wq_plane[:, 0:P],
+                rhs=wq_codes[:].bitcast(FP8X4),
+                rhs_scale=wq_plane[:],
+                start=True,
+                stop=True,
+            )
         for h, j in banks:
             xq_pass(h, j)
         quantize_wa(0)
@@ -161,7 +172,7 @@ def tile_mix_peak_of_mixed_sum_kernel(
         for g in range(2):
             for j in range(2):
                 xt_pass(g, 0, j)
-        for h, j in banks[2:-1]:
+        for h, j in banks[2:]:
             for g in range(2):
                 xt_pass(g, h, j)
 
@@ -209,24 +220,32 @@ def tile_mix_peak_of_mixed_sum_kernel(
                 start=True,
                 stop=True,
             )
-        for g in range(2):
-            xt_pass(g, 1, TILES - 1)
         pair(0, 2)
         pair(1, 0)
 
-        half_g = sbuf("half_g", [P, TILES, B], F32)
+        partial = sbuf("partial", [P, TILES, B], F32)
         result = sbuf("result", [P, TILES, B], F32)
-        nc.scalar.activation(half_g[:], gsum[:], ACT.Copy, scale=0.5)
 
-        def finish(j):
-            nc.vector.scalar_tensor_tensor(
-                out=result[:, j, :], in0=peaks[:, j, :], scalar=neg_mean[:, TILES + j : TILES + j + 1],
-                in1=half_g[:, j, :], op0=ALU.add, op1=ALU.add,
-            )
+        def mean_of(j):
+            return neg_mean[:, TILES + j : TILES + j + 1]
+
+        def store(j):
             nc.sync.dma_start(out=out[j * P : (j + 1) * P, :], in_=result[:, j, :])
 
-        for j in (2, 3):
-            peak(1, j)
-            total(1, j)
-        for j in range(TILES):
-            finish(j)
+        peak(1, 2)
+        total(1, 3)
+        nc.vector.scalar_tensor_tensor(
+            out=partial[:, 0:2, :], in0=gsum[:, 0:2, :], scalar=0.5, in1=peaks[:, 0:2, :], op0=ALU.mult, op1=ALU.add
+        )
+        nc.scalar.activation(partial[:, 2:4, :], gsum[:, 2:4, :], ACT.Copy, scale=0.5)
+        peak(1, 3)
+        total(1, 2)
+        for j in (0, 1):
+            nc.vector.tensor_scalar_add(result[:, j, :], partial[:, j, :], mean_of(j))
+            store(j)
+        for j in (3, 2):
+            nc.vector.scalar_tensor_tensor(
+                out=result[:, j, :], in0=peaks[:, j, :], scalar=mean_of(j), in1=partial[:, j, :],
+                op0=ALU.add, op1=ALU.add,
+            )
+            store(j)

@@ -21,7 +21,8 @@ GROUP = T // B
 HALF = 512
 TILES = N // P
 N_HALF = N // 2
-V_COLS = 336
+V_COLS = 304
+QUANT_SPANS = ((0, 128), (128, 256), (256, 512))
 XT_ROW = 4
 G_ROW = 8
 WARM_PASSES = 3
@@ -83,16 +84,14 @@ def tile_mix_peak_of_mixed_sum_kernel(
         wa_raw = [sbuf("wa_raw%d" % g, [P, PACK, N], F32) for g in range(2)]
         xt_w = as_words(xt_words)
 
-        nc.sync.dma_start(out=wa_raw[0][:, 0:2, :], in_=wa_rows[0][:, 0:2, :])
-        load_scales(nc.sync, 0, 4)
         wq_codes = load_words("wq_codes", as_words(wq_words)[0])
         xq_codes = sbuf("xq_codes", [P, 2 * T], U8)
         nc.sync.dma_start(out=xq_codes[:].bitcast(I32), in_=xq_words[0].bitcast(I32))
-        nc.sync.dma_start(out=wa_raw[0][:, 2:4, :], in_=wa_rows[0][:, 2:4, :])
+        load_scales(nc.sync, 0, 4)
+        nc.sync.dma_start(out=wa_raw[0][:], in_=wa_rows[0])
         load_scales(nc.sync, 4, 8)
         nc.sync.dma_start(out=wa_raw[1][:], in_=wa_rows[1])
         load_scales(nc.gpsimd, 8, 12)
-        load_scales(nc.sync, 16, 20)
         xt00 = load_words("xt00", xt_w[0][:, 0:HALF])
         xt10 = load_words("xt10", xt_w[1][:, 0:HALF])
         xt_h1 = sbuf("xt_h1", [P, 2, HALF], U32)
@@ -100,6 +99,7 @@ def tile_mix_peak_of_mixed_sum_kernel(
         load_scales(nc.sync, 12, 16)
         wg_codes = load_words("wg_codes", as_words(wg_words)[0])
         xg_codes = load_words("xg_codes", as_words(xg_words)[0])
+        load_scales(nc.sync, 16, 20)
         xt_codes = {(0, 0): xt00[:], (1, 0): xt10[:], (0, 1): xt_h1[:, 0, :], (1, 1): xt_h1[:, 1, :]}
 
         wa_codes, wa_plane = {}, {}
@@ -113,17 +113,20 @@ def tile_mix_peak_of_mixed_sum_kernel(
                     wa_raw[g][:, :, c0:c1].rearrange("p j (c i) -> p c j i", i=4),
                 )
 
-            nc.vector.tensor_copy(*views(0, N_HALF))
+            nc.vector.tensor_copy(*views(0, P))
             nc.scalar.copy(*views(V_COLS, N))
-            nc.vector.tensor_copy(*views(N_HALF, V_COLS))
-            for u in range(2):
-                wa_codes[g, u] = sbuf("wa_codes%d%d" % (g, u), [P, N_HALF], U32)
-                wa_plane[g, u] = sbuf("wa_plane%d%d" % (g, u), [P, N_HALF], U8)
+            nc.vector.tensor_copy(*views(P, V_COLS))
+            for c0, c1 in QUANT_SPANS:
+                codes = sbuf("wa_codes%d_%d" % (g, c0), [P, c1 - c0], U32)
+                plane = sbuf("wa_plane%d_%d" % (g, c0), [P, c1 - c0], U8)
                 nc.vector.quantize_mx(
-                    out=wa_codes[g, u][:].bitcast(FP8X4),
-                    scales=wa_plane[g, u][:],
-                    in_=grouped[:, u * N_HALF : (u + 1) * N_HALF, :].rearrange("p c j -> p (c j)"),
+                    out=codes[:].bitcast(FP8X4),
+                    scales=plane[:],
+                    in_=grouped[:, c0:c1, :].rearrange("p c j -> p (c j)"),
                 )
+                for c in range(c0, c1, P):
+                    wa_codes[g, c // P] = codes[:, c - c0 : c - c0 + P]
+                    wa_plane[g, c // P] = plane[:, c - c0 : c - c0 + P]
 
         banks = [(h, j) for h in range(2) for j in range(TILES)]
         z = {}
@@ -143,12 +146,11 @@ def tile_mix_peak_of_mixed_sum_kernel(
             )
 
         def xt_pass(g, h, j):
-            u, c0 = divmod(j * P, N_HALF)
             t0 = g * T + h * HALF
             nc.tensor.matmul_mx(
                 out=z[h, j][:],
-                lhsT=wa_codes[g, u][:, c0 : c0 + P].bitcast(FP8X4),
-                lhsT_scale=wa_plane[g, u][:, c0 : c0 + P],
+                lhsT=wa_codes[g, j].bitcast(FP8X4),
+                lhsT_scale=wa_plane[g, j],
                 rhs=xt_codes[g, h].bitcast(FP8X4),
                 rhs_scale=xt_plane[XT_ROW:P, t0 : t0 + HALF],
                 start=False,
@@ -201,13 +203,11 @@ def tile_mix_peak_of_mixed_sum_kernel(
                     accum_out=neg_mean[:, i : i + 1],
                 )
 
-        def pair(h, j):
+        def drain(h, j):
             peak(h, j)
-            total(h, j + 1)
-            peak(h, j + 1)
             total(h, j)
 
-        pair(0, 0)
+        drain(0, 0)
         gsum = ps.tile([P, TILES, B], F32, name="gsum", tag="bank00")
         for j in range(TILES):
             cols = slice(j * P, (j + 1) * P)
@@ -220,8 +220,8 @@ def tile_mix_peak_of_mixed_sum_kernel(
                 start=True,
                 stop=True,
             )
-        pair(0, 2)
-        pair(1, 0)
+        for h, j in banks[1:-1]:
+            drain(h, j)
 
         partial = sbuf("partial", [P, TILES, B], F32)
         result = sbuf("result", [P, TILES, B], F32)
@@ -232,20 +232,20 @@ def tile_mix_peak_of_mixed_sum_kernel(
         def store(j):
             nc.sync.dma_start(out=out[j * P : (j + 1) * P, :], in_=result[:, j, :])
 
-        peak(1, 2)
-        total(1, 3)
-        nc.vector.scalar_tensor_tensor(
-            out=partial[:, 0:2, :], in0=gsum[:, 0:2, :], scalar=0.5, in1=peaks[:, 0:2, :], op0=ALU.mult, op1=ALU.add
-        )
-        nc.scalar.activation(partial[:, 2:4, :], gsum[:, 2:4, :], ACT.Copy, scale=0.5)
-        peak(1, 3)
-        total(1, 2)
-        for j in (0, 1):
+        def add_half_g(j0, j1):
+            nc.vector.scalar_tensor_tensor(
+                out=partial[:, j0:j1, :], in0=gsum[:, j0:j1, :], scalar=0.5, in1=peaks[:, j0:j1, :],
+                op0=ALU.mult, op1=ALU.add,
+            )
+
+        def finish(j):
             nc.vector.tensor_scalar_add(result[:, j, :], partial[:, j, :], mean_of(j))
             store(j)
-        for j in (3, 2):
-            nc.vector.scalar_tensor_tensor(
-                out=result[:, j, :], in0=peaks[:, j, :], scalar=mean_of(j), in1=partial[:, j, :],
-                op0=ALU.add, op1=ALU.add,
-            )
-            store(j)
+
+        add_half_g(0, 2)
+        drain(1, 3)
+        finish(0)
+        finish(1)
+        add_half_g(2, 4)
+        finish(2)
+        finish(3)

from contextlib import ExitStack

import concourse.mybir as mybir

K, L, M, T, B, N = 1024, 512, 512, 1024, 128, 512
FLOPS = 2 * N * T * (K + L) + 2 * N * B * M

F32 = mybir.dt.float32
BF16 = mybir.dt.bfloat16
I32 = mybir.dt.int32
U32 = mybir.dt.uint32
U8 = mybir.dt.uint8
FP8X4 = mybir.dt.float8_e4m3fn_x4
FP4X4 = mybir.dt.float4_e2m1fn_x4
ALU = mybir.AluOpType
ACT = mybir.ActivationFunctionType

P = 128
PACK = 4
GROUP = T // B
HALF = 512
TILES = N // P
N_HALF = N // 2
V_COLS = 304
QUANT_SPANS = ((0, 128), (128, 256), (256, 512))
XT_ROW = 4
G_ROW = 8
WARM_PASSES = 3


def tile_mix_peak_of_mixed_sum_kernel(
    tc, xt_words, xt_scales, wa, xq_words, xq_scales, wq_words, wq_scales,
    xg_words, xg_scales, wg_words, wg_scales, out,
):
    nc = tc.nc
    with ExitStack() as ctx:
        sb = ctx.enter_context(tc.tile_pool(name="sb", bufs=1))
        ps = ctx.enter_context(tc.psum_pool(name="ps", bufs=1))
        ctx.enter_context(tc.manual_schedule())

        def sbuf(name, shape, dtype):
            return sb.tile(shape, dtype, name=name, align_bytes=64)

        wq_plane = sbuf("wq_plane", [P, N], U8)
        xq_plane = sbuf("xq_plane", [P, T], U8)
        xt_plane = sbuf("xt_plane", [P, 2 * T], U8)
        wg_plane = sbuf("wg_plane", [P, N], U8)
        xg_plane = sbuf("xg_plane", [P, B], U8)
        for plane in (wq_plane, xt_plane, xq_plane, xg_plane, wg_plane):
            nc.vector.memset(plane[:].bitcast(I32), 0)

        warm_in = sbuf("warm_in", [P, 1], F32)
        warm_out = sbuf("warm_out", [P, 1], F32)
        nc.gpsimd.memset(warm_in[:], 0.0)
        nc.scalar.activation(warm_out[:], warm_in[:], ACT.Copy)

        def scale_rows(plane, scales, first_row):
            passes = scales.shape[0]
            rows = scales.bitcast(I32).rearrange("g (q r) c -> r q g c", r=4)
            dst = plane[:].bitcast(I32).rearrange("p (g c) -> p g c", g=passes)
            return [(dst[first_row + r : P : 32], rows[r]) for r in range(4)]

        scale_loads = (
            scale_rows(wq_plane, wq_scales, 0)
            + scale_rows(xq_plane, xq_scales, 0)
            + scale_rows(xt_plane, xt_scales, XT_ROW)
            + scale_rows(wg_plane, wg_scales, G_ROW)
            + scale_rows(xg_plane, xg_scales, G_ROW)
        )

        def load_scales(engine, first, last):
            for dst, src in scale_loads[first:last]:
                engine.dma_start(out=dst, in_=src)

        def load_words(name, words):
            t = sbuf(name, [P, words.shape[1]], U32)
            nc.sync.dma_start(out=t[:].bitcast(I32), in_=words)
            return t

        def as_words(words):
            return words.rearrange("g p c r -> g p (c r)").bitcast(I32)

        wa_rows = wa.rearrange("(g p j) n -> g p j n", p=P, j=PACK)
        wa_raw = [sbuf("wa_raw%d" % g, [P, PACK, N], F32) for g in range(2)]
        xt_w = as_words(xt_words)

        wq_codes = load_words("wq_codes", as_words(wq_words)[0])
        xq_codes = sbuf("xq_codes", [P, 2 * T], U8)
        nc.sync.dma_start(out=xq_codes[:].bitcast(I32), in_=xq_words[0].bitcast(I32))
        load_scales(nc.sync, 0, 4)
        nc.sync.dma_start(out=wa_raw[0][:], in_=wa_rows[0])
        load_scales(nc.sync, 4, 8)
        nc.sync.dma_start(out=wa_raw[1][:], in_=wa_rows[1])
        load_scales(nc.gpsimd, 8, 12)
        xt00 = load_words("xt00", xt_w[0][:, 0:HALF])
        xt10 = load_words("xt10", xt_w[1][:, 0:HALF])
        xt_h1 = sbuf("xt_h1", [P, 2, HALF], U32)
        nc.sync.dma_start(out=xt_h1[:].bitcast(I32), in_=xt_w.rearrange("g p c -> p g c")[:, :, HALF:T])
        load_scales(nc.sync, 12, 16)
        wg_codes = load_words("wg_codes", as_words(wg_words)[0])
        xg_codes = load_words("xg_codes", as_words(xg_words)[0])
        load_scales(nc.sync, 16, 20)
        xt_codes = {(0, 0): xt00[:], (1, 0): xt10[:], (0, 1): xt_h1[:, 0, :], (1, 1): xt_h1[:, 1, :]}

        wa_codes, wa_plane = {}, {}

        def quantize_wa(g):
            grouped = sbuf("wa_bf16_%d" % g, [P, N, PACK], BF16)

            def views(c0, c1):
                return (
                    grouped[:, c0:c1, :].rearrange("p (c i) j -> p c j i", i=4),
                    wa_raw[g][:, :, c0:c1].rearrange("p j (c i) -> p c j i", i=4),
                )

            nc.vector.tensor_copy(*views(0, P))
            nc.scalar.copy(*views(V_COLS, N))
            nc.vector.tensor_copy(*views(P, V_COLS))
            for c0, c1 in QUANT_SPANS:
                codes = sbuf("wa_codes%d_%d" % (g, c0), [P, c1 - c0], U32)
                plane = sbuf("wa_plane%d_%d" % (g, c0), [P, c1 - c0], U8)
                nc.vector.quantize_mx(
                    out=codes[:].bitcast(FP8X4),
                    scales=plane[:],
                    in_=grouped[:, c0:c1, :].rearrange("p c j -> p (c j)"),
                )
                for c in range(c0, c1, P):
                    wa_codes[g, c // P] = codes[:, c - c0 : c - c0 + P]
                    wa_plane[g, c // P] = plane[:, c - c0 : c - c0 + P]

        banks = [(h, j) for h in range(2) for j in range(TILES)]
        z = {}
        for h, j in banks:
            z[h, j] = ps.tile([P, HALF], F32, name="z%d%d" % (h, j), tag="bank%d%d" % (h, j))

        def xq_pass(h, j):
            cols = slice(j * P, (j + 1) * P)
            nc.tensor.matmul_mx(
                out=z[h, j][:],
                lhsT=wq_codes[:, cols].bitcast(FP8X4),
                lhsT_scale=wq_plane[:, cols],
                rhs=xq_codes[:, 2 * h * HALF : 2 * (h + 1) * HALF].bitcast(FP4X4),
                rhs_scale=xq_plane[:, h * HALF : (h + 1) * HALF],
                start=True,
                stop=False,
            )

        def xt_pass(g, h, j):
            t0 = g * T + h * HALF
            nc.tensor.matmul_mx(
                out=z[h, j][:],
                lhsT=wa_codes[g, j].bitcast(FP8X4),
                lhsT_scale=wa_plane[g, j],
                rhs=xt_codes[g, h].bitcast(FP8X4),
                rhs_scale=xt_plane[XT_ROW:P, t0 : t0 + HALF],
                start=False,
                stop=(g == 1),
            )

        for h, j in banks[-WARM_PASSES:]:
            nc.tensor.matmul_mx(
                out=z[h, j][:],
                lhsT=wq_codes[:, 0:P].bitcast(FP8X4),
                lhsT_scale=wq_plane[:, 0:P],
                rhs=wq_codes[:].bitcast(FP8X4),
                rhs_scale=wq_plane[:],
                start=True,
                stop=True,
            )
        for h, j in banks:
            xq_pass(h, j)
        quantize_wa(0)
        quantize_wa(1)
        for g in range(2):
            for j in range(2):
                xt_pass(g, 0, j)
        for h, j in banks[2:]:
            for g in range(2):
                xt_pass(g, h, j)

        peaks = sbuf("peaks", [P, TILES, B], F32)
        neg_mean = sbuf("neg_mean", [P, 2 * TILES], F32)
        scaled = sbuf("scaled", [P, 2 * TILES, HALF], BF16)
        groups = HALF // GROUP

        def peak(h, j):
            nc.vector.tensor_reduce(
                out=peaks[:, j, h * groups : (h + 1) * groups],
                in_=z[h, j][:].rearrange("p (b e) -> p b e", e=GROUP),
                axis=mybir.AxisListType.X,
                op=ALU.max,
            )

        def total(h, j):
            i = h * TILES + j
            if h == 0:
                nc.scalar.activation(
                    scaled[:, i, :], z[h, j][:], ACT.Copy, scale=-1.0 / (T * HALF), accum_out=neg_mean[:, i : i + 1]
                )
            else:
                nc.scalar.activation(
                    scaled[:, i, :], z[h, j][:], ACT.Identity, scale=-1.0 / T, bias=neg_mean[:, j : j + 1],
                    accum_out=neg_mean[:, i : i + 1],
                )

        def drain(h, j):
            peak(h, j)
            total(h, j)

        drain(0, 0)
        gsum = ps.tile([P, TILES, B], F32, name="gsum", tag="bank00")
        for j in range(TILES):
            cols = slice(j * P, (j + 1) * P)
            nc.tensor.matmul_mx(
                out=gsum[:, j, :],
                lhsT=wg_codes[:, cols].bitcast(FP8X4),
                lhsT_scale=wg_plane[G_ROW:P, cols],
                rhs=xg_codes[:].bitcast(FP8X4),
                rhs_scale=xg_plane[G_ROW:P, :],
                start=True,
                stop=True,
            )
        for h, j in banks[1:-1]:
            drain(h, j)

        partial = sbuf("partial", [P, TILES, B], F32)
        result = sbuf("result", [P, TILES, B], F32)

        def mean_of(j):
            return neg_mean[:, TILES + j : TILES + j + 1]

        def store(j):
            nc.sync.dma_start(out=out[j * P : (j + 1) * P, :], in_=result[:, j, :])

        def add_half_g(j0, j1):
            nc.vector.scalar_tensor_tensor(
                out=partial[:, j0:j1, :], in0=gsum[:, j0:j1, :], scalar=0.5, in1=peaks[:, j0:j1, :],
                op0=ALU.mult, op1=ALU.add,
            )

        def finish(j):
            nc.vector.tensor_scalar_add(result[:, j, :], partial[:, j, :], mean_of(j))
            store(j)

        add_half_g(0, 2)
        drain(1, 3)
        finish(0)
        finish(1)
        add_half_g(2, 4)
        finish(2)
        finish(3)
